import numpy as np
import ml_dtypes


def mxq(x, axis, fmt="e4m3"):
    dtype, down = {"e4m3": (ml_dtypes.float8_e4m3fn, 7), "e5m2": (ml_dtypes.float8_e5m2, 14)}[fmt]
    v = np.moveaxis(np.asarray(x, np.float32).astype(ml_dtypes.bfloat16).astype(np.float64), axis, -1)
    blocks = v.reshape(v.shape[:-1] + (-1, 32))
    amax = np.abs(blocks).max(-1, keepdims=True)
    byte = np.maximum(np.where(amax > 0, np.frexp(amax)[1] - 1 + 127, 0) - down, 1)
    scale = np.exp2(byte - 127.0)
    codes = (blocks / scale).astype(np.float32).astype(dtype).astype(np.float64)
    return np.moveaxis((codes * scale).reshape(v.shape), -1, axis)


WIDE = False


def mx_kscale(k):
    if not WIDE:
        return np.ones(k)
    levels = np.array([10, -10, 5, -5, 0])
    if k % 512:
        return np.exp2(np.random.permutation(np.resize(levels, k // 32))).repeat(32)
    a = np.empty((k // 512, 16))
    for p in range(k // 512):
        a[p, :8] = np.random.permutation(np.resize(levels, 8))
        for g in range(8):
            far = levels[np.abs(levels - a[p, g]) >= 10]
            a[p, g + 8] = far[np.random.randint(len(far))]
    return np.exp2(a.ravel()).repeat(32)


def f64(x):
    return np.asarray(x).astype(np.float64)


def striped(idx):
    return np.tile(np.asarray(idx).reshape(-1, 16).T, (8, 1)).astype(np.uint16)


def unstriped(offs):
    return offs[:16].T.reshape(-1).astype(np.int64)


E2M1 = np.array([0.0, 0.5, 1.0, 1.5, 2.0, 3.0, 4.0, 6.0, -0.0, -0.5, -1.0, -1.5, -2.0, -3.0, -4.0, -6.0])


def pack_weight(w, fmt):
    k, n = w.shape
    w = f64(np.asarray(w, np.float32).astype(ml_dtypes.bfloat16)).reshape(k // 32, 32, n)
    amax = np.abs(w).max(1)
    if fmt == "e4m3":
        byte = np.frexp(amax)[1] - 1 + 127 - 7
    else:
        mant, ex = np.frexp(amax / 6.0)
        byte = np.where(mant > 0.5, ex, ex - 1) + 127
    byte = np.clip(np.where(amax > 0, byte, 1), 1, 254)
    scaled = (w * np.exp2(127.0 - byte)[:, None, :]).reshape(k, n).astype(np.float32)
    by_word = np.ascontiguousarray(scaled.reshape(k // 512, 128, 4, n).transpose(0, 1, 3, 2))
    if fmt == "e4m3":
        words = by_word.astype(ml_dtypes.float8_e4m3fn).view(np.uint8)
    else:
        c = by_word.astype(ml_dtypes.float4_e2m1fn).view(np.uint8) & 0xF
        words = (c[..., 0::2] | (c[..., 1::2] << 4)).reshape(k // 512, 128, 2 * n)
    return np.ascontiguousarray(words), np.ascontiguousarray(byte.astype(np.uint8).reshape(k // 512, 16, n))


def unpack_weight(words, scales, fmt):
    g, _, n = scales.shape
    words = np.ascontiguousarray(words).reshape(g, 128, n, -1)
    if fmt == "e4m3":
        vals = words.view(ml_dtypes.float8_e4m3fn).astype(np.float64)
    else:
        nib = np.empty((g, 128, n, 4), np.uint8)
        nib[..., 0::2] = words & 0xF
        nib[..., 1::2] = words >> 4
        vals = E2M1[nib]
    vals = vals * np.repeat(np.exp2(scales.astype(np.float64) - 127.0), 8, axis=1)[..., None]
    return vals.transpose(0, 1, 3, 2).reshape(g * 512, n)


D, E, T, I, G, U, Q = 512, 512, 4096, 1024, 64, 512, 128


def setup_inputs():
    n = np.random.standard_normal
    idx = np.random.permutation(T)[:I]
    idx2 = np.random.permutation(U)[:G]
    fd = mx_kscale(D)
    fe = mx_kscale(E)
    keysp = pack_weight(n((D, T)) / fd[:, None], "e4m3")
    valsp = pack_weight(n((E, T)) / fe[:, None], "e4m3")
    return {
        "query": (n((D, Q)) * 0.6 / np.sqrt(D) * fd[:, None]).astype(np.float32),
        "keys_words": keysp[0],
        "keys_scales": keysp[1],
        "gout": (n((E, Q)) * 1 / np.sqrt(E) * fe[:, None]).astype(np.float32),
        "vals_words": valsp[0],
        "vals_scales": valsp[1],
        "old": (np.random.uniform(0.0, 8.0, (Q, U))).astype(np.float32),
        "fade": (np.random.uniform(0.5, 1.0, (1, U))).astype(np.float32),
        "offs": striped(idx),
        "offs2": striped(idx2),
    }


def reference(query, keys_words, keys_scales, gout, vals_words, vals_scales, old, fade, offs, offs2):
    idx = unstriped(offs)
    idx2 = unstriped(offs2)
    keysu = unpack_weight(keys_words, keys_scales, "e4m3")
    valsu = unpack_weight(vals_words, vals_scales, "e4m3")
    queryq = mxq(f64(query), 0, "e4m3")
    keysidxg = keysu[:, idx]
    a = queryq.T @ keysidxg
    goutq = mxq(f64(gout), 0, "e4m3")
    valsidxg = valsu[:, idx]
    dp = goutq.T @ valsidxg
    p = np.exp(a - np.max(a, axis=1, keepdims=True))
    sg = (p * np.abs(dp)).reshape(Q, G, I // G).sum(axis=2) / np.sum(p, axis=1, keepdims=True) * 512.0
    sf = np.zeros((Q, U))
    sf[:, idx2] = sg
    y = f64(old) * f64(fade) + sf
    return y

@@ -1,0 +1,179 @@
+from contextlib import ExitStack
+
+import concourse.mybir as mybir
+from concourse.masks import make_identity
+
+D, E, T, I, G, U, Q = 512, 512, 4096, 1024, 64, 512, 128
+FLOPS = 2 * Q * I * (D + E)
+
+F32 = mybir.dt.float32
+BF16 = mybir.dt.bfloat16
+I32 = mybir.dt.int32
+U32 = mybir.dt.uint32
+U16 = mybir.dt.uint16
+U8 = mybir.dt.uint8
+FP8X4 = mybir.dt.float8_e4m3fn_x4
+ALU = mybir.AluOpType
+ACT = mybir.ActivationFunctionType
+AXIS_X = mybir.AxisListType.X
+
+P = 128
+PACK = 4
+HALF = 512
+HALVES = I // HALF
+PAGE = I // G
+LIST_COLS = HALF // 16
+ROW_STEP = 8
+BLOCKS = U // P
+
+
+def tile_attend_pagesaliency_kernel(
+    tc, query, keys_words, keys_scales, gout, vals_words, vals_scales, old, fade, offs, offs2, out
+):
+    nc = tc.nc
+    with ExitStack() as ctx:
+        sb = ctx.enter_context(tc.tile_pool(name="sb", bufs=1))
+        ps = ctx.enter_context(tc.psum_pool(name="ps", bufs=1))
+
+        slots = sb.tile([P, I // 16], U16, name="slots")
+        pages = sb.tile([P, G // 16], U16, name="pages")
+        k_bytes = sb.tile([P, T], U8, name="k_bytes")
+        v_bytes = sb.tile([P, T], U8, name="v_bytes", tag="v_bytes_then_keys", align_bytes=64)
+        k_words = sb.tile([P, T], I32, name="k_words")
+        v_words = sb.tile([P, T], I32, name="v_words")
+        q_raw = sb.tile([P, PACK, Q], F32, name="q_raw")
+        g_raw = sb.tile([P, PACK, Q], F32, name="g_raw")
+
+        nc.vector.memset(k_bytes[:].bitcast(I32), 0)
+        nc.vector.memset(v_bytes[:].bitcast(I32), 0)
+
+        nc.sync.dma_start(slots[:], offs)
+        nc.sync.dma_start(pages[:], offs2)
+        nc.sync.dma_start(q_raw[:], query.rearrange("(p t) q -> p t q", t=PACK))
+        nc.sync.dma_start(g_raw[:], gout.rearrange("(p t) q -> p t q", t=PACK))
+        nc.sync.dma_start(k_words[:], keys_words[0].rearrange("p n t -> p (n t)").bitcast(I32))
+        nc.sync.dma_start(v_words[:], vals_words[0].rearrange("p n t -> p (n t)").bitcast(I32))
+        nc.scalar.dma_start(k_bytes[0:P:ROW_STEP, :].bitcast(I32), keys_scales[0].bitcast(I32))
+        nc.scalar.dma_start(v_bytes[4:P:ROW_STEP, :].bitcast(I32), vals_scales[0].bitcast(I32))
+
+        k_plane = sb.tile([P, I], U8, name="k_plane", align_bytes=64)
+        v_plane = sb.tile([P, I], U8, name="v_plane", align_bytes=64)
+        placed = sb.tile([P, U], F32, name="placed")
+        ident = sb.tile([P, P], F32, name="ident")
+        nc.vector.memset(k_plane[:].bitcast(I32), 0)
+        nc.vector.memset(v_plane[:].bitcast(I32), 0)
+        nc.vector.memset(placed[:], 0.0)
+        nc.vector.memset(ident[:], 0.0)
+        make_identity(nc, ident[:], nomemset=True)
+        fade_rows = sb.tile([P, P], F32, name="fade_rows")
+        nc.vector.memset(fade_rows[:], 0.0)
+        nc.gpsimd.dma_start(fade_rows[0:BLOCKS, :], fade.rearrange("o (c p) -> (o c) p", p=P))
+        fade_turned = ps.tile([P, P], F32, name="fade_turned")
+        nc.tensor.transpose(fade_turned[:], fade_rows[:], ident[:])
+        fade_col = sb.tile([P, BLOCKS], F32, name="fade_col")
+
+        grouped = sb.tile([P, 2, Q, PACK], BF16, name="grouped", align_bytes=64)
+        nc.scalar.copy(grouped[:, 0], q_raw[:].rearrange("p t q -> p q t"))
+        nc.scalar.copy(grouped[:, 1], g_raw[:].rearrange("p t q -> p q t"))
+
+        nc.scalar.copy(fade_col[:], fade_turned[:, 0:BLOCKS])
+
+        k_picked = sb.tile([P, I], U8, name="k_picked", tag="k_picked_then_old")
+        nc.vector.tensor_copy(k_picked[:], k_bytes[:].indirect(slots[:]))
+        for j in range(4):
+            nc.scalar.dma_start(
+                k_plane[j:P:32, :].bitcast(I32), k_picked[ROW_STEP * j : P : 32, :].bitcast(I32)
+            )
+        old_sb = sb.tile([P, U], F32, name="old_sb", tag="k_picked_then_old")
+        nc.sync.dma_start(old_sb[:], old)
+
+        v_picked = sb.tile([P, I], U8, name="v_picked")
+        nc.vector.tensor_copy(v_picked[:], v_bytes[:].indirect(slots[:]))
+        for j in range(4):
+            nc.gpsimd.dma_start(
+                v_plane[j:P:32, :].bitcast(I32), v_picked[ROW_STEP * j + 4 : P : 32, :].bitcast(I32)
+            )
+
+        codes = sb.tile([P, 2, Q], U32, name="codes", align_bytes=64)
+        scales = sb.tile([P, 2, Q], U8, name="scales", align_bytes=64)
+        nc.vector.quantize_mx(
+            out=codes[:].rearrange("p a q -> p (a q)").bitcast(FP8X4),
+            scales=scales[:].rearrange("p a q -> p (a q)"),
+            in_=grouped[:].rearrange("p a q t -> p (a q t)"),
+        )
+
+        def product(which, words, picked_all, plane, h, name):
+            picked = picked_all[:, h * HALF : (h + 1) * HALF]
+            nc.vector.tensor_copy(
+                picked, words[:].bitcast(U32).indirect(slots[:, h * LIST_COLS : (h + 1) * LIST_COLS])
+            )
+            bank = ps.tile([P, HALF], F32, name=name + "_bank")
+            nc.tensor.matmul_mx(
+                out=bank[:],
+                lhsT=codes[:, which, :].bitcast(FP8X4),
+                lhsT_scale=scales[:, which, :],
+                rhs=picked.bitcast(FP8X4),
+                rhs_scale=plane[:, h * HALF : (h + 1) * HALF],
+                start=True,
+                stop=True,
+            )
+            return bank
+
+        keys_picked = sb.tile([P, I], U32, name="keys_picked", tag="v_bytes_then_keys", align_bytes=64)
+        score = [product(0, k_words, keys_picked, k_plane, h, "score%d" % h) for h in range(HALVES)]
+        half_max = sb.tile([P, HALVES], F32, name="half_max", tag="half_max_then_vals", align_bytes=64)
+        for h in range(HALVES):
+            nc.vector.tensor_reduce(half_max[:, h : h + 1], score[h][:], AXIS_X, ALU.max)
+        neg_max = sb.tile([P, 1], F32, name="neg_max")
+        nc.vector.tensor_reduce(neg_max[:], half_max[:], AXIS_X, ALU.max, negate=True)
+
+        prob = sb.tile([P, I], F32, name="prob")
+        half_sum = sb.tile([P, HALVES], F32, name="half_sum", tag="half_sum_then_faded")
+        for h in range(HALVES):
+            nc.scalar.activation(
+                prob[:, h * HALF : (h + 1) * HALF],
+                score[h][:],
+                ACT.Exp,
+                bias=neg_max[:],
+                accum_out=half_sum[:, h : h + 1],
+            )
+        row_sum = sb.tile([P, 1], F32, name="row_sum")
+        nc.scalar.activation(row_sum[:], half_sum[:, 0:1], ACT.Identity, bias=half_sum[:, 1:2])
+
+        vals_picked = sb.tile([P, I], U32, name="vals_picked", tag="half_max_then_vals", align_bytes=64)
+        grad = [product(1, v_words, vals_picked, v_plane, h, "grad%d" % h) for h in range(HALVES)]
+
+        inv_sum = sb.tile([P, 1], F32, name="inv_sum")
+        nc.vector.reciprocal(inv_sum[:], row_sum[:])
+        norm = sb.tile([P, G], F32, name="norm")
+        nc.scalar.activation(norm[:], inv_sum[:].to_broadcast([P, G]), ACT.Copy, scale=512.0)
+
+        turned = ps.tile([P, BLOCKS, Q], F32, name="turned")
+        for c in range(BLOCKS):
+            nc.tensor.transpose(turned[:, c, :], old_sb[:, c * P : (c + 1) * P], ident[:])
+        faded_t = sb.tile([P, BLOCKS, Q], F32, name="faded_t", tag="half_sum_then_faded")
+        for c in range(BLOCKS):
+            nc.scalar.activation(faded_t[:, c, :], turned[:, c, :], ACT.Copy, scale=fade_col[:, c : c + 1])
+        faded = ps.tile([P, U], F32, name="faded")
+        for c in range(BLOCKS):
+            nc.tensor.transpose(faded[:, c * P : (c + 1) * P], faded_t[:, c, :], ident[:])
+
+        lean = sb.tile([P, I], F32, name="lean")
+        for h in range(HALVES):
+            cols = slice(h * HALF, (h + 1) * HALF)
+            nc.vector.tensor_tensor(lean[:, cols], grad[h][:], prob[:, cols], ALU.mult)
+        page_sum = sb.tile([P, G], F32, name="page_sum")
+        for h in range(HALVES):
+            nc.vector.tensor_reduce(
+                page_sum[:, h * (G // HALVES) : (h + 1) * (G // HALVES)],
+                lean[:, h * HALF : (h + 1) * HALF].rearrange("p (g i) -> p g i", i=PAGE),
+                AXIS_X,
+                ALU.add,
+                apply_absolute_value=True,
+            )
+        nc.vector.tensor_tensor(placed[:].indirect(pages[:]), page_sum[:], norm[:], ALU.mult)
+
+        result = sb.tile([P, U], F32, name="result")
+        for queue, cols in ((nc.sync, slice(0, U // 2)), (nc.scalar, slice(U // 2, U))):
+            nc.vector.tensor_tensor(result[:, cols], placed[:, cols], faded[:, cols], ALU.add)
+            queue.dma_start(out[:, cols], result[:, cols])

@@ -23,7 +23,9 @@ HALF = 512
 HALVES = I // HALF
 PAGE = I // G
 LIST_COLS = HALF // 16
-ROW_STEP = 8
+ROWS = 16
+K_ROW = 112
+V_ROW = 48
 BLOCKS = U // P
 
 
@@ -37,61 +39,39 @@ def tile_attend_pagesaliency_kernel(
 
         slots = sb.tile([P, I // 16], U16, name="slots")
         pages = sb.tile([P, G // 16], U16, name="pages")
-        k_bytes = sb.tile([P, T], U8, name="k_bytes")
-        v_bytes = sb.tile([P, T], U8, name="v_bytes", tag="v_bytes_then_keys", align_bytes=64)
+        k_bytes = sb.tile([P, T], U8, name="k_bytes", tag="k_bytes_then_placed")
+        v_bytes = sb.tile([P, T], U8, name="v_bytes", tag="v_bytes_then_old")
         k_words = sb.tile([P, T], I32, name="k_words")
-        v_words = sb.tile([P, T], I32, name="v_words")
-        q_raw = sb.tile([P, PACK, Q], F32, name="q_raw")
-        g_raw = sb.tile([P, PACK, Q], F32, name="g_raw")
-
-        nc.vector.memset(k_bytes[:].bitcast(I32), 0)
-        nc.vector.memset(v_bytes[:].bitcast(I32), 0)
+        fade_rows = sb.tile([P, P], F32, name="fade_rows")
+        q_raw = sb.tile([P, PACK, Q], F32, name="q_raw", tag="q_raw_then_ident")
+        g_raw = sb.tile([P, PACK, Q], F32, name="g_raw", tag="g_raw_then_v_picked")
 
         nc.sync.dma_start(slots[:], offs)
-        nc.sync.dma_start(pages[:], offs2)
+        nc.sync.dma_start(k_bytes[K_ROW : K_ROW + ROWS, :].bitcast(I32), keys_scales[0].bitcast(I32))
+        nc.sync.dma_start(v_bytes[V_ROW : V_ROW + ROWS, :].bitcast(I32), vals_scales[0].bitcast(I32))
         nc.sync.dma_start(q_raw[:], query.rearrange("(p t) q -> p t q", t=PACK))
         nc.sync.dma_start(g_raw[:], gout.rearrange("(p t) q -> p t q", t=PACK))
         nc.sync.dma_start(k_words[:], keys_words[0].rearrange("p n t -> p (n t)").bitcast(I32))
-        nc.sync.dma_start(v_words[:], vals_words[0].rearrange("p n t -> p (n t)").bitcast(I32))
-        nc.scalar.dma_start(k_bytes[0:P:ROW_STEP, :].bitcast(I32), keys_scales[0].bitcast(I32))
-        nc.scalar.dma_start(v_bytes[4:P:ROW_STEP, :].bitcast(I32), vals_scales[0].bitcast(I32))
+        nc.sync.dma_start(pages[:], offs2)
+        nc.sync.dma_start(fade_rows[P - BLOCKS : P, :], fade.rearrange("o (c p) -> (o c) p", p=P))
 
-        k_plane = sb.tile([P, I], U8, name="k_plane", align_bytes=64)
-        v_plane = sb.tile([P, I], U8, name="v_plane", align_bytes=64)
-        placed = sb.tile([P, U], F32, name="placed")
-        ident = sb.tile([P, P], F32, name="ident")
-        nc.vector.memset(k_plane[:].bitcast(I32), 0)
-        nc.vector.memset(v_plane[:].bitcast(I32), 0)
-        nc.vector.memset(placed[:], 0.0)
-        nc.vector.memset(ident[:], 0.0)
-        make_identity(nc, ident[:], nomemset=True)
-        fade_rows = sb.tile([P, P], F32, name="fade_rows")
-        nc.vector.memset(fade_rows[:], 0.0)
-        nc.gpsimd.dma_start(fade_rows[0:BLOCKS, :], fade.rearrange("o (c p) -> (o c) p", p=P))
-        fade_turned = ps.tile([P, P], F32, name="fade_turned")
-        nc.tensor.transpose(fade_turned[:], fade_rows[:], ident[:])
-        fade_col = sb.tile([P, BLOCKS], F32, name="fade_col")
+        nc.vector.memset(k_bytes[0:K_ROW, :].bitcast(I32), 0)
+        nc.vector.memset(v_bytes[0:V_ROW, :].bitcast(I32), 0)
+        nc.vector.memset(v_bytes[V_ROW + ROWS : P, :].bitcast(I32), 0)
 
-        grouped = sb.tile([P, 2, Q, PACK], BF16, name="grouped", align_bytes=64)
+        planes = sb.tile([P, I], U8, name="planes", align_bytes=64)
+        nc.vector.memset(planes[:].bitcast(I32), 0)
+
+        grouped = sb.tile([P, 2, Q, PACK], BF16, name="grouped", tag="grouped_then_vals", align_bytes=64)
         nc.scalar.copy(grouped[:, 0], q_raw[:].rearrange("p t q -> p q t"))
         nc.scalar.copy(grouped[:, 1], g_raw[:].rearrange("p t q -> p q t"))
 
-        nc.scalar.copy(fade_col[:], fade_turned[:, 0:BLOCKS])
-
-        k_picked = sb.tile([P, I], U8, name="k_picked", tag="k_picked_then_old")
+        k_picked = sb.tile([P, I], U8, name="k_picked")
         nc.vector.tensor_copy(k_picked[:], k_bytes[:].indirect(slots[:]))
-        for j in range(4):
-            nc.scalar.dma_start(
-                k_plane[j:P:32, :].bitcast(I32), k_picked[ROW_STEP * j : P : 32, :].bitcast(I32)
-            )
-        old_sb = sb.tile([P, U], F32, name="old_sb", tag="k_picked_then_old")
-        nc.sync.dma_start(old_sb[:], old)
-
-        v_picked = sb.tile([P, I], U8, name="v_picked")
-        nc.vector.tensor_copy(v_picked[:], v_bytes[:].indirect(slots[:]))
-        for j in range(4):
-            nc.gpsimd.dma_start(
-                v_plane[j:P:32, :].bitcast(I32), v_picked[ROW_STEP * j + 4 : P : 32, :].bitcast(I32)
+        for quad in range(4):
+            nc.sync.dma_start(
+                planes[32 * quad : 32 * quad + 4, :].bitcast(I32),
+                k_picked[K_ROW + 4 * quad : K_ROW + 4 * quad + 4, :].bitcast(I32),
             )
 
         codes = sb.tile([P, 2, Q], U32, name="codes", align_bytes=64)
@@ -102,12 +82,29 @@ def tile_attend_pagesaliency_kernel(
             in_=grouped[:].rearrange("p a q t -> p (a q t)"),
         )
 
+        v_words = sb.tile([P, T], I32, name="v_words", tag="grouped_then_vals", align_bytes=64)
+        nc.sync.dma_start(v_words[:], vals_words[0].rearrange("p n t -> p (n t)").bitcast(I32))
+
+        v_picked = sb.tile([P, I], U8, name="v_picked", tag="g_raw_then_v_picked")
+        nc.vector.tensor_copy(v_picked[:], v_bytes[:].indirect(slots[:]))
+        old_sb = sb.tile([P, U], F32, name="old_sb", tag="v_bytes_then_old")
+        nc.sync.dma_start(old_sb[:], old)
+
+        ident = sb.tile([P, P], F32, name="ident", tag="q_raw_then_ident")
+        nc.vector.memset(ident[:], 0.0)
+        make_identity(nc, ident[:], nomemset=True)
+        nc.vector.memset(fade_rows[0 : P - BLOCKS, :], 0.0)
+        fade_turned = ps.tile([P, P], F32, name="fade_turned")
+        nc.tensor.transpose(fade_turned[:], fade_rows[:], ident[:])
+        fade_col = sb.tile([P, BLOCKS], F32, name="fade_col", tag="fade_col_then_norm")
+        nc.scalar.copy(fade_col[:], fade_turned[:, P - BLOCKS : P])
+
         def product(which, words, picked_all, plane, h, name):
             picked = picked_all[:, h * HALF : (h + 1) * HALF]
             nc.vector.tensor_copy(
                 picked, words[:].bitcast(U32).indirect(slots[:, h * LIST_COLS : (h + 1) * LIST_COLS])
             )
-            bank = ps.tile([P, HALF], F32, name=name + "_bank")
+            bank = ps.tile([P, HALF], F32, name=name + "_bank", tag=name)
             nc.tensor.matmul_mx(
                 out=bank[:],
                 lhsT=codes[:, which, :].bitcast(FP8X4),
@@ -119,8 +116,13 @@ def tile_attend_pagesaliency_kernel(
             )
             return bank
 
-        keys_picked = sb.tile([P, I], U32, name="keys_picked", tag="v_bytes_then_keys", align_bytes=64)
-        score = [product(0, k_words, keys_picked, k_plane, h, "score%d" % h) for h in range(HALVES)]
+        keys_picked = sb.tile([P, I], U32, name="keys_picked", align_bytes=64)
+        score = [product(0, k_words, keys_picked, planes[:], h, "score%d" % h) for h in range(HALVES)]
+        for quad in range(4):
+            nc.sync.dma_start(
+                planes[32 * quad + 4 : 32 * quad + 8, :].bitcast(I32),
+                v_picked[V_ROW + 4 * quad : V_ROW + 4 * quad + 4, :].bitcast(I32),
+            )
         half_max = sb.tile([P, HALVES], F32, name="half_max", tag="half_max_then_vals", align_bytes=64)
         for h in range(HALVES):
             nc.vector.tensor_reduce(half_max[:, h : h + 1], score[h][:], AXIS_X, ALU.max)
@@ -140,28 +142,29 @@ def tile_attend_pagesaliency_kernel(
         row_sum = sb.tile([P, 1], F32, name="row_sum")
         nc.scalar.activation(row_sum[:], half_sum[:, 0:1], ACT.Identity, bias=half_sum[:, 1:2])
 
-        vals_picked = sb.tile([P, I], U32, name="vals_picked", tag="half_max_then_vals", align_bytes=64)
-        grad = [product(1, v_words, vals_picked, v_plane, h, "grad%d" % h) for h in range(HALVES)]
-
-        inv_sum = sb.tile([P, 1], F32, name="inv_sum")
-        nc.vector.reciprocal(inv_sum[:], row_sum[:])
-        norm = sb.tile([P, G], F32, name="norm")
-        nc.scalar.activation(norm[:], inv_sum[:].to_broadcast([P, G]), ACT.Copy, scale=512.0)
-
         turned = ps.tile([P, BLOCKS, Q], F32, name="turned")
         for c in range(BLOCKS):
             nc.tensor.transpose(turned[:, c, :], old_sb[:, c * P : (c + 1) * P], ident[:])
         faded_t = sb.tile([P, BLOCKS, Q], F32, name="faded_t", tag="half_sum_then_faded")
         for c in range(BLOCKS):
             nc.scalar.activation(faded_t[:, c, :], turned[:, c, :], ACT.Copy, scale=fade_col[:, c : c + 1])
-        faded = ps.tile([P, U], F32, name="faded")
-        for c in range(BLOCKS):
-            nc.tensor.transpose(faded[:, c * P : (c + 1) * P], faded_t[:, c, :], ident[:])
+
+        vals_picked = sb.tile([P, I], U32, name="vals_picked", tag="half_max_then_vals", align_bytes=64)
+        grad = [product(1, v_words, vals_picked, planes[4:P], h, "grad%d" % h) for h in range(HALVES)]
+
+        inv_sum = sb.tile([P, 1], F32, name="inv_sum", tag="grouped_then_vals", align_bytes=64)
+        nc.vector.reciprocal(inv_sum[:], row_sum[:])
+        norm = sb.tile([P, G], F32, name="norm", tag="fade_col_then_norm")
+        nc.scalar.activation(norm[:], inv_sum[:].to_broadcast([P, G]), ACT.Copy, scale=512.0)
 
         lean = sb.tile([P, I], F32, name="lean")
         for h in range(HALVES):
             cols = slice(h * HALF, (h + 1) * HALF)
             nc.vector.tensor_tensor(lean[:, cols], grad[h][:], prob[:, cols], ALU.mult)
+        faded = ps.tile([P, U], F32, name="faded", tag="grad0")
+        for c in range(BLOCKS):
+            nc.tensor.transpose(faded[:, c * P : (c + 1) * P], faded_t[:, c, :], ident[:])
+
         page_sum = sb.tile([P, G], F32, name="page_sum")
         for h in range(HALVES):
             nc.vector.tensor_reduce(
@@ -171,6 +174,8 @@ def tile_attend_pagesaliency_kernel(
                 ALU.add,
                 apply_absolute_value=True,
             )
+        placed = sb.tile([P, U], F32, name="placed", tag="k_bytes_then_placed")
+        nc.vector.memset(placed[:], 0.0)
         nc.vector.tensor_tensor(placed[:].indirect(pages[:]), page_sum[:], norm[:], ALU.mult)
 
         result = sb.tile([P, U], F32, name="result")

@@ -27,6 +27,7 @@ ROWS = 16
 K_ROW = 112
 V_ROW = 48
 BLOCKS = U // P
+GRAD_COLS = (slice(0, 512), slice(512, 768), slice(768, 1024))
 
 
 def tile_attend_pagesaliency_kernel(
@@ -39,11 +40,11 @@ def tile_attend_pagesaliency_kernel(
 
         slots = sb.tile([P, I // 16], U16, name="slots")
         pages = sb.tile([P, G // 16], U16, name="pages")
-        k_bytes = sb.tile([P, T], U8, name="k_bytes", tag="k_bytes_then_placed")
+        k_bytes = sb.tile([P, T], U8, name="k_bytes")
         v_bytes = sb.tile([P, T], U8, name="v_bytes", tag="v_bytes_then_old")
         k_words = sb.tile([P, T], I32, name="k_words")
         fade_rows = sb.tile([P, P], F32, name="fade_rows")
-        q_raw = sb.tile([P, PACK, Q], F32, name="q_raw", tag="q_raw_then_ident")
+        q_raw = sb.tile([P, PACK, Q], F32, name="q_raw")
         g_raw = sb.tile([P, PACK, Q], F32, name="g_raw", tag="g_raw_then_v_picked")
 
         nc.sync.dma_start(slots[:], offs)
@@ -56,11 +57,16 @@ def tile_attend_pagesaliency_kernel(
         nc.sync.dma_start(fade_rows[P - BLOCKS : P, :], fade.rearrange("o (c p) -> (o c) p", p=P))
 
         nc.vector.memset(k_bytes[0:K_ROW, :].bitcast(I32), 0)
-        nc.vector.memset(v_bytes[0:V_ROW, :].bitcast(I32), 0)
-        nc.vector.memset(v_bytes[V_ROW + ROWS : P, :].bitcast(I32), 0)
 
+        ident = sb.tile([P, P], F32, name="ident")
         planes = sb.tile([P, I], U8, name="planes", align_bytes=64)
-        nc.vector.memset(planes[:].bitcast(I32), 0)
+        placed = sb.tile([P, U], F32, name="placed")
+        make_identity(nc, ident[:])
+        nc.gpsimd.memset(planes[:].bitcast(I32), 0)
+        nc.gpsimd.memset(v_bytes[V_ROW + ROWS : P, :].bitcast(I32), 0)
+        nc.gpsimd.memset(v_bytes[0:V_ROW, :].bitcast(I32), 0)
+        nc.gpsimd.memset(placed[:], 0.0)
+        nc.gpsimd.memset(fade_rows[0 : P - BLOCKS, :], 0.0)
 
         grouped = sb.tile([P, 2, Q, PACK], BF16, name="grouped", tag="grouped_then_vals", align_bytes=64)
         nc.scalar.copy(grouped[:, 0], q_raw[:].rearrange("p t q -> p q t"))
@@ -90,53 +96,57 @@ def tile_attend_pagesaliency_kernel(
         old_sb = sb.tile([P, U], F32, name="old_sb", tag="v_bytes_then_old")
         nc.sync.dma_start(old_sb[:], old)
 
-        ident = sb.tile([P, P], F32, name="ident", tag="q_raw_then_ident")
-        nc.vector.memset(ident[:], 0.0)
-        make_identity(nc, ident[:], nomemset=True)
-        nc.vector.memset(fade_rows[0 : P - BLOCKS, :], 0.0)
         fade_turned = ps.tile([P, P], F32, name="fade_turned")
         nc.tensor.transpose(fade_turned[:], fade_rows[:], ident[:])
         fade_col = sb.tile([P, BLOCKS], F32, name="fade_col", tag="fade_col_then_norm")
         nc.scalar.copy(fade_col[:], fade_turned[:, P - BLOCKS : P])
 
-        def product(which, words, picked_all, plane, h, name):
-            picked = picked_all[:, h * HALF : (h + 1) * HALF]
+        def gather_words(picked, words, h):
             nc.vector.tensor_copy(
-                picked, words[:].bitcast(U32).indirect(slots[:, h * LIST_COLS : (h + 1) * LIST_COLS])
+                picked[:, h * HALF : (h + 1) * HALF],
+                words[:].bitcast(U32).indirect(slots[:, h * LIST_COLS : (h + 1) * LIST_COLS]),
             )
-            bank = ps.tile([P, HALF], F32, name=name + "_bank", tag=name)
+
+        def product(which, picked, plane, cols, name):
+            bank = ps.tile([P, cols.stop - cols.start], F32, name=name, tag=name)
             nc.tensor.matmul_mx(
                 out=bank[:],
                 lhsT=codes[:, which, :].bitcast(FP8X4),
                 lhsT_scale=scales[:, which, :],
-                rhs=picked.bitcast(FP8X4),
-                rhs_scale=plane[:, h * HALF : (h + 1) * HALF],
+                rhs=picked[:, cols].bitcast(FP8X4),
+                rhs_scale=plane[:, cols],
                 start=True,
                 stop=True,
             )
             return bank
 
         keys_picked = sb.tile([P, I], U32, name="keys_picked", align_bytes=64)
-        score = [product(0, k_words, keys_picked, planes[:], h, "score%d" % h) for h in range(HALVES)]
+        score = []
+        for h in range(HALVES):
+            gather_words(keys_picked, k_words, h)
+            score.append(product(0, keys_picked, planes[:], slice(h * HALF, (h + 1) * HALF), "score%d" % h))
         for quad in range(4):
             nc.sync.dma_start(
                 planes[32 * quad + 4 : 32 * quad + 8, :].bitcast(I32),
                 v_picked[V_ROW + 4 * quad : V_ROW + 4 * quad + 4, :].bitcast(I32),
             )
-        half_max = sb.tile([P, HALVES], F32, name="half_max", tag="half_max_then_vals", align_bytes=64)
-        for h in range(HALVES):
-            nc.vector.tensor_reduce(half_max[:, h : h + 1], score[h][:], AXIS_X, ALU.max)
+        neg_max0 = sb.tile([P, 1], F32, name="neg_max0", tag="neg_max0_then_vals", align_bytes=64)
+        nc.vector.tensor_reduce(neg_max0[:], score[0][:], AXIS_X, ALU.max, negate=True)
+        neg_score1 = sb.tile([P, HALF], F32, name="neg_score1")
         neg_max = sb.tile([P, 1], F32, name="neg_max")
-        nc.vector.tensor_reduce(neg_max[:], half_max[:], AXIS_X, ALU.max, negate=True)
+        nc.vector.tensor_scalar(
+            neg_score1[:], score[1][:], -1.0, neg_max0[:], ALU.mult, ALU.min, accum_out=neg_max[:]
+        )
 
         prob = sb.tile([P, I], F32, name="prob")
         half_sum = sb.tile([P, HALVES], F32, name="half_sum", tag="half_sum_then_faded")
-        for h in range(HALVES):
+        for h, (source, sign) in enumerate(((score[0], 1.0), (neg_score1, -1.0))):
             nc.scalar.activation(
                 prob[:, h * HALF : (h + 1) * HALF],
-                score[h][:],
+                source[:],
                 ACT.Exp,
                 bias=neg_max[:],
+                scale=sign,
                 accum_out=half_sum[:, h : h + 1],
             )
         row_sum = sb.tile([P, 1], F32, name="row_sum")
@@ -149,8 +159,12 @@ def tile_attend_pagesaliency_kernel(
         for c in range(BLOCKS):
             nc.scalar.activation(faded_t[:, c, :], turned[:, c, :], ACT.Copy, scale=fade_col[:, c : c + 1])
 
-        vals_picked = sb.tile([P, I], U32, name="vals_picked", tag="half_max_then_vals", align_bytes=64)
-        grad = [product(1, v_words, vals_picked, planes[4:P], h, "grad%d" % h) for h in range(HALVES)]
+        vals_picked = sb.tile([P, I], U32, name="vals_picked", tag="neg_max0_then_vals", align_bytes=64)
+        for h in range(HALVES):
+            gather_words(vals_picked, v_words, h)
+        grad = [
+            product(1, vals_picked, planes[4:P], cols, "grad%d" % n) for n, cols in enumerate(GRAD_COLS)
+        ]
 
         inv_sum = sb.tile([P, 1], F32, name="inv_sum", tag="grouped_then_vals", align_bytes=64)
         nc.vector.reciprocal(inv_sum[:], row_sum[:])
@@ -158,9 +172,8 @@ def tile_attend_pagesaliency_kernel(
         nc.scalar.activation(norm[:], inv_sum[:].to_broadcast([P, G]), ACT.Copy, scale=512.0)
 
         lean = sb.tile([P, I], F32, name="lean")
-        for h in range(HALVES):
-            cols = slice(h * HALF, (h + 1) * HALF)
-            nc.vector.tensor_tensor(lean[:, cols], grad[h][:], prob[:, cols], ALU.mult)
+        for bank, cols in zip(grad, GRAD_COLS):
+            nc.vector.tensor_tensor(lean[:, cols], bank[:], prob[:, cols], ALU.mult)
         faded = ps.tile([P, U], F32, name="faded", tag="grad0")
         for c in range(BLOCKS):
             nc.tensor.transpose(faded[:, c * P : (c + 1) * P], faded_t[:, c, :], ident[:])
@@ -174,8 +187,6 @@ def tile_attend_pagesaliency_kernel(
                 ALU.add,
                 apply_absolute_value=True,
             )
-        placed = sb.tile([P, U], F32, name="placed", tag="k_bytes_then_placed")
-        nc.vector.memset(placed[:], 0.0)
         nc.vector.tensor_tensor(placed[:].indirect(pages[:]), page_sum[:], norm[:], ALU.mult)
 
         result = sb.tile([P, U], F32, name="result")

@@ -59,12 +59,14 @@ def tile_attend_pagesaliency_kernel(
         nc.vector.memset(k_bytes[0:K_ROW, :].bitcast(I32), 0)
 
         ident = sb.tile([P, P], F32, name="ident")
-        planes = sb.tile([P, I], U8, name="planes", align_bytes=64)
+        k_plane = sb.tile([P, I], U8, name="k_plane", align_bytes=64)
+        v_plane = sb.tile([P, I], U8, name="v_plane", align_bytes=64)
         placed = sb.tile([P, U], F32, name="placed")
         make_identity(nc, ident[:])
-        nc.gpsimd.memset(planes[:].bitcast(I32), 0)
+        nc.gpsimd.memset(k_plane[:].bitcast(I32), 0)
         nc.gpsimd.memset(v_bytes[V_ROW + ROWS : P, :].bitcast(I32), 0)
         nc.gpsimd.memset(v_bytes[0:V_ROW, :].bitcast(I32), 0)
+        nc.gpsimd.memset(v_plane[:].bitcast(I32), 0)
         nc.gpsimd.memset(placed[:], 0.0)
         nc.gpsimd.memset(fade_rows[0 : P - BLOCKS, :], 0.0)
 
@@ -76,7 +78,7 @@ def tile_attend_pagesaliency_kernel(
         nc.vector.tensor_copy(k_picked[:], k_bytes[:].indirect(slots[:]))
         for quad in range(4):
             nc.sync.dma_start(
-                planes[32 * quad : 32 * quad + 4, :].bitcast(I32),
+                k_plane[32 * quad : 32 * quad + 4, :].bitcast(I32),
                 k_picked[K_ROW + 4 * quad : K_ROW + 4 * quad + 4, :].bitcast(I32),
             )
 
@@ -95,6 +97,11 @@ def tile_attend_pagesaliency_kernel(
         nc.vector.tensor_copy(v_picked[:], v_bytes[:].indirect(slots[:]))
         old_sb = sb.tile([P, U], F32, name="old_sb", tag="v_bytes_then_old")
         nc.sync.dma_start(old_sb[:], old)
+        for quad in range(4):
+            nc.sync.dma_start(
+                v_plane[32 * quad : 32 * quad + 4, :].bitcast(I32),
+                v_picked[V_ROW + 4 * quad : V_ROW + 4 * quad + 4, :].bitcast(I32),
+            )
 
         fade_turned = ps.tile([P, P], F32, name="fade_turned")
         nc.tensor.transpose(fade_turned[:], fade_rows[:], ident[:])
@@ -124,12 +131,7 @@ def tile_attend_pagesaliency_kernel(
         score = []
         for h in range(HALVES):
             gather_words(keys_picked, k_words, h)
-            score.append(product(0, keys_picked, planes[:], slice(h * HALF, (h + 1) * HALF), "score%d" % h))
-        for quad in range(4):
-            nc.sync.dma_start(
-                planes[32 * quad + 4 : 32 * quad + 8, :].bitcast(I32),
-                v_picked[V_ROW + 4 * quad : V_ROW + 4 * quad + 4, :].bitcast(I32),
-            )
+            score.append(product(0, keys_picked, k_plane, slice(h * HALF, (h + 1) * HALF), "score%d" % h))
         neg_max0 = sb.tile([P, 1], F32, name="neg_max0", tag="neg_max0_then_vals", align_bytes=64)
         nc.vector.tensor_reduce(neg_max0[:], score[0][:], AXIS_X, ALU.max, negate=True)
         neg_score1 = sb.tile([P, HALF], F32, name="neg_score1")
@@ -163,7 +165,7 @@ def tile_attend_pagesaliency_kernel(
         for h in range(HALVES):
             gather_words(vals_picked, v_words, h)
         grad = [
-            product(1, vals_picked, planes[4:P], cols, "grad%d" % n) for n, cols in enumerate(GRAD_COLS)
+            product(1, vals_picked, v_plane, cols, "grad%d" % n) for n, cols in enumerate(GRAD_COLS)
         ]
 
         inv_sum = sb.tile([P, 1], F32, name="inv_sum", tag="grouped_then_vals", align_bytes=64)

from contextlib import ExitStack

import concourse.mybir as mybir
from concourse.masks import make_identity

D, E, T, I, G, U, Q = 512, 512, 4096, 1024, 64, 512, 128
FLOPS = 2 * Q * I * (D + E)

F32 = mybir.dt.float32
BF16 = mybir.dt.bfloat16
I32 = mybir.dt.int32
U32 = mybir.dt.uint32
U16 = mybir.dt.uint16
U8 = mybir.dt.uint8
FP8X4 = mybir.dt.float8_e4m3fn_x4
ALU = mybir.AluOpType
ACT = mybir.ActivationFunctionType
AXIS_X = mybir.AxisListType.X

P = 128
PACK = 4
HALF = 512
HALVES = I // HALF
PAGE = I // G
LIST_COLS = HALF // 16
ROWS = 16
K_ROW = 112
V_ROW = 48
BLOCKS = U // P
GRAD_COLS = (slice(0, 512), slice(512, 768), slice(768, 1024))


def tile_attend_pagesaliency_kernel(
    tc, query, keys_words, keys_scales, gout, vals_words, vals_scales, old, fade, offs, offs2, out
):
    nc = tc.nc
    with ExitStack() as ctx:
        sb = ctx.enter_context(tc.tile_pool(name="sb", bufs=1))
        ps = ctx.enter_context(tc.psum_pool(name="ps", bufs=1))

        slots = sb.tile([P, I // 16], U16, name="slots")
        pages = sb.tile([P, G // 16], U16, name="pages")
        k_bytes = sb.tile([P, T], U8, name="k_bytes")
        v_bytes = sb.tile([P, T], U8, name="v_bytes", tag="v_bytes_then_old")
        k_words = sb.tile([P, T], I32, name="k_words")
        fade_rows = sb.tile([P, P], F32, name="fade_rows")
        q_raw = sb.tile([P, PACK, Q], F32, name="q_raw")
        g_raw = sb.tile([P, PACK, Q], F32, name="g_raw", tag="g_raw_then_v_picked")

        nc.sync.dma_start(slots[:], offs)
        nc.sync.dma_start(k_bytes[K_ROW : K_ROW + ROWS, :].bitcast(I32), keys_scales[0].bitcast(I32))
        nc.sync.dma_start(v_bytes[V_ROW : V_ROW + ROWS, :].bitcast(I32), vals_scales[0].bitcast(I32))
        nc.sync.dma_start(q_raw[:], query.rearrange("(p t) q -> p t q", t=PACK))
        nc.sync.dma_start(g_raw[:], gout.rearrange("(p t) q -> p t q", t=PACK))
        nc.sync.dma_start(k_words[:], keys_words[0].rearrange("p n t -> p (n t)").bitcast(I32))
        nc.sync.dma_start(pages[:], offs2)
        nc.sync.dma_start(fade_rows[P - BLOCKS : P, :], fade.rearrange("o (c p) -> (o c) p", p=P))

        nc.vector.memset(k_bytes[0:K_ROW, :].bitcast(I32), 0)

        ident = sb.tile([P, P], F32, name="ident")
        k_plane = sb.tile([P, I], U8, name="k_plane", align_bytes=64)
        v_plane = sb.tile([P, I], U8, name="v_plane", align_bytes=64)
        placed = sb.tile([P, U], F32, name="placed")
        make_identity(nc, ident[:])
        nc.gpsimd.memset(k_plane[:].bitcast(I32), 0)
        nc.gpsimd.memset(v_bytes[V_ROW + ROWS : P, :].bitcast(I32), 0)
        nc.gpsimd.memset(v_bytes[0:V_ROW, :].bitcast(I32), 0)
        nc.gpsimd.memset(v_plane[:].bitcast(I32), 0)
        nc.gpsimd.memset(placed[:], 0.0)
        nc.gpsimd.memset(fade_rows[0 : P - BLOCKS, :], 0.0)

        grouped = sb.tile([P, 2, Q, PACK], BF16, name="grouped", tag="grouped_then_vals", align_bytes=64)
        nc.scalar.copy(grouped[:, 0], q_raw[:].rearrange("p t q -> p q t"))
        nc.scalar.copy(grouped[:, 1], g_raw[:].rearrange("p t q -> p q t"))

        k_picked = sb.tile([P, I], U8, name="k_picked")
        nc.vector.tensor_copy(k_picked[:], k_bytes[:].indirect(slots[:]))
        for quad in range(4):
            nc.sync.dma_start(
                k_plane[32 * quad : 32 * quad + 4, :].bitcast(I32),
                k_picked[K_ROW + 4 * quad : K_ROW + 4 * quad + 4, :].bitcast(I32),
            )

        codes = sb.tile([P, 2, Q], U32, name="codes", align_bytes=64)
        scales = sb.tile([P, 2, Q], U8, name="scales", align_bytes=64)
        nc.vector.quantize_mx(
            out=codes[:].rearrange("p a q -> p (a q)").bitcast(FP8X4),
            scales=scales[:].rearrange("p a q -> p (a q)"),
            in_=grouped[:].rearrange("p a q t -> p (a q t)"),
        )

        v_words = sb.tile([P, T], I32, name="v_words", tag="grouped_then_vals", align_bytes=64)
        nc.sync.dma_start(v_words[:], vals_words[0].rearrange("p n t -> p (n t)").bitcast(I32))

        v_picked = sb.tile([P, I], U8, name="v_picked", tag="g_raw_then_v_picked")
        nc.vector.tensor_copy(v_picked[:], v_bytes[:].indirect(slots[:]))
        old_sb = sb.tile([P, U], F32, name="old_sb", tag="v_bytes_then_old")
        nc.sync.dma_start(old_sb[:], old)
        for quad in range(4):
            nc.sync.dma_start(
                v_plane[32 * quad : 32 * quad + 4, :].bitcast(I32),
                v_picked[V_ROW + 4 * quad : V_ROW + 4 * quad + 4, :].bitcast(I32),
            )

        fade_turned = ps.tile([P, P], F32, name="fade_turned")
        nc.tensor.transpose(fade_turned[:], fade_rows[:], ident[:])
        fade_col = sb.tile([P, BLOCKS], F32, name="fade_col", tag="fade_col_then_norm")
        nc.scalar.copy(fade_col[:], fade_turned[:, P - BLOCKS : P])

        def gather_words(picked, words, h):
            nc.vector.tensor_copy(
                picked[:, h * HALF : (h + 1) * HALF],
                words[:].bitcast(U32).indirect(slots[:, h * LIST_COLS : (h + 1) * LIST_COLS]),
            )

        def product(which, picked, plane, cols, name):
            bank = ps.tile([P, cols.stop - cols.start], F32, name=name, tag=name)
            nc.tensor.matmul_mx(
                out=bank[:],
                lhsT=codes[:, which, :].bitcast(FP8X4),
                lhsT_scale=scales[:, which, :],
                rhs=picked[:, cols].bitcast(FP8X4),
                rhs_scale=plane[:, cols],
                start=True,
                stop=True,
            )
            return bank

        keys_picked = sb.tile([P, I], U32, name="keys_picked", align_bytes=64)
        score = []
        for h in range(HALVES):
            gather_words(keys_picked, k_words, h)
            score.append(product(0, keys_picked, k_plane, slice(h * HALF, (h + 1) * HALF), "score%d" % h))
        neg_max0 = sb.tile([P, 1], F32, name="neg_max0", tag="neg_max0_then_vals", align_bytes=64)
        nc.vector.tensor_reduce(neg_max0[:], score[0][:], AXIS_X, ALU.max, negate=True)
        neg_score1 = sb.tile([P, HALF], F32, name="neg_score1")
        neg_max = sb.tile([P, 1], F32, name="neg_max")
        nc.vector.tensor_scalar(
            neg_score1[:], score[1][:], -1.0, neg_max0[:], ALU.mult, ALU.min, accum_out=neg_max[:]
        )

        prob = sb.tile([P, I], F32, name="prob")
        half_sum = sb.tile([P, HALVES], F32, name="half_sum", tag="half_sum_then_faded")
        for h, (source, sign) in enumerate(((score[0], 1.0), (neg_score1, -1.0))):
            nc.scalar.activation(
                prob[:, h * HALF : (h + 1) * HALF],
                source[:],
                ACT.Exp,
                bias=neg_max[:],
                scale=sign,
                accum_out=half_sum[:, h : h + 1],
            )
        row_sum = sb.tile([P, 1], F32, name="row_sum")
        nc.scalar.activation(row_sum[:], half_sum[:, 0:1], ACT.Identity, bias=half_sum[:, 1:2])

        turned = ps.tile([P, BLOCKS, Q], F32, name="turned")
        for c in range(BLOCKS):
            nc.tensor.transpose(turned[:, c, :], old_sb[:, c * P : (c + 1) * P], ident[:])
        faded_t = sb.tile([P, BLOCKS, Q], F32, name="faded_t", tag="half_sum_then_faded")
        for c in range(BLOCKS):
            nc.scalar.activation(faded_t[:, c, :], turned[:, c, :], ACT.Copy, scale=fade_col[:, c : c + 1])

        vals_picked = sb.tile([P, I], U32, name="vals_picked", tag="neg_max0_then_vals", align_bytes=64)
        for h in range(HALVES):
            gather_words(vals_picked, v_words, h)
        grad = [
            product(1, vals_picked, v_plane, cols, "grad%d" % n) for n, cols in enumerate(GRAD_COLS)
        ]

        inv_sum = sb.tile([P, 1], F32, name="inv_sum", tag="grouped_then_vals", align_bytes=64)
        nc.vector.reciprocal(inv_sum[:], row_sum[:])
        norm = sb.tile([P, G], F32, name="norm", tag="fade_col_then_norm")
        nc.scalar.activation(norm[:], inv_sum[:].to_broadcast([P, G]), ACT.Copy, scale=512.0)

        lean = sb.tile([P, I], F32, name="lean")
        for bank, cols in zip(grad, GRAD_COLS):
            nc.vector.tensor_tensor(lean[:, cols], bank[:], prob[:, cols], ALU.mult)
        faded = ps.tile([P, U], F32, name="faded", tag="grad0")
        for c in range(BLOCKS):
            nc.tensor.transpose(faded[:, c * P : (c + 1) * P], faded_t[:, c, :], ident[:])

        page_sum = sb.tile([P, G], F32, name="page_sum")
        for h in range(HALVES):
            nc.vector.tensor_reduce(
                page_sum[:, h * (G // HALVES) : (h + 1) * (G // HALVES)],
                lean[:, h * HALF : (h + 1) * HALF].rearrange("p (g i) -> p g i", i=PAGE),
                AXIS_X,
                ALU.add,
                apply_absolute_value=True,
            )
        nc.vector.tensor_tensor(placed[:].indirect(pages[:]), page_sum[:], norm[:], ALU.mult)

        result = sb.tile([P, U], F32, name="result")
        for queue, cols in ((nc.sync, slice(0, U // 2)), (nc.scalar, slice(U // 2, U))):
            nc.vector.tensor_tensor(result[:, cols], placed[:, cols], faded[:, cols], ALU.add)
            queue.dma_start(out[:, cols], result[:, cols])
